import numpy as np
import ml_dtypes


def mxq(x, axis, fmt="e4m3"):
    dtype, down = {"e4m3": (ml_dtypes.float8_e4m3fn, 7), "e5m2": (ml_dtypes.float8_e5m2, 14)}[fmt]
    v = np.moveaxis(np.asarray(x, np.float32).astype(ml_dtypes.bfloat16).astype(np.float64), axis, -1)
    blocks = v.reshape(v.shape[:-1] + (-1, 32))
    amax = np.abs(blocks).max(-1, keepdims=True)
    byte = np.maximum(np.where(amax > 0, np.frexp(amax)[1] - 1 + 127, 0) - down, 1)
    scale = np.exp2(byte - 127.0)
    codes = (blocks / scale).astype(np.float32).astype(dtype).astype(np.float64)
    return np.moveaxis((codes * scale).reshape(v.shape), -1, axis)


WIDE = False


def mx_kscale(k):
    if not WIDE:
        return np.ones(k)
    levels = np.array([24, -24, 12, -12, 0])
    if k % 512:
        return np.exp2(np.random.permutation(np.resize(levels, k // 32))).repeat(32)
    a = np.empty((k // 512, 16))
    for p in range(k // 512):
        a[p, :8] = np.random.permutation(np.resize(levels, 8))
        for g in range(8):
            far = levels[np.abs(levels - a[p, g]) >= 10]
            a[p, g + 8] = far[np.random.randint(len(far))]
    return np.exp2(a.ravel()).repeat(32)


def f64(x):
    return np.asarray(x).astype(np.float64)


def striped(idx):
    return np.tile(idx.reshape(-1, 16).T, (8, 1)).astype(np.uint16)


def unstriped(offs):
    return offs[:16].T.reshape(-1).astype(np.int64)


def striped8(idx):
    return np.concatenate([v.reshape(-1, 16).T for v in idx]).astype(np.uint16)


def unstriped8(offs):
    return np.stack([offs[16 * g:16 * g + 16].T.reshape(-1) for g in range(8)]).astype(np.int64)


E2M1 = np.array([0.0, 0.5, 1.0, 1.5, 2.0, 3.0, 4.0, 6.0, -0.0, -0.5, -1.0, -1.5, -2.0, -3.0, -4.0, -6.0])


def pack_weight(w, fmt):
    k, n = w.shape
    w = f64(np.asarray(w, np.float32).astype(ml_dtypes.bfloat16)).reshape(k // 32, 32, n)
    amax = np.abs(w).max(1)
    if fmt == "e4m3":
        byte = np.frexp(amax)[1] - 1 + 127 - 7
    else:
        mant, ex = np.frexp(amax / 6.0)
        byte = np.where(mant > 0.5, ex, ex - 1) + 127
    byte = np.clip(np.where(amax > 0, byte, 1), 1, 254)
    scaled = (w * np.exp2(127.0 - byte)[:, None, :]).reshape(k, n).astype(np.float32)
    by_word = np.ascontiguousarray(scaled.reshape(k // 512, 128, 4, n).transpose(0, 1, 3, 2))
    if fmt == "e4m3":
        words = by_word.astype(ml_dtypes.float8_e4m3fn).view(np.uint8)
    else:
        c = by_word.astype(ml_dtypes.float4_e2m1fn).view(np.uint8) & 0xF
        words = (c[..., 0::2] | (c[..., 1::2] << 4)).reshape(k // 512, 128, 2 * n)
    return np.ascontiguousarray(words), np.ascontiguousarray(byte.astype(np.uint8).reshape(k // 512, 16, n))


def unpack_weight(words, scales, fmt):
    g, _, n = scales.shape
    words = np.ascontiguousarray(words).reshape(g, 128, n, -1)
    if fmt == "e4m3":
        vals = words.view(ml_dtypes.float8_e4m3fn).astype(np.float64)
    else:
        nib = np.empty((g, 128, n, 4), np.uint8)
        nib[..., 0::2] = words & 0xF
        nib[..., 1::2] = words >> 4
        vals = E2M1[nib]
    vals = vals * np.repeat(np.exp2(scales.astype(np.float64) - 127.0), 8, axis=1)[..., None]
    return vals.transpose(0, 1, 3, 2).reshape(g * 512, n)


K, L, R, N, T, J = 512, 512, 512, 512, 2048, 1024


def setup_inputs():
    n = np.random.standard_normal
    s = mx_kscale(K)[:, None]
    s2 = mx_kscale(L)[:, None]
    u = mx_kscale(R)[:, None]
    p_tab = pack_weight(n((L, T)) * s2, "e4m3")
    p_wa = pack_weight(n((K, R)) / np.sqrt(K) / s * u.T, "e4m3")
    p_wb = pack_weight(n((L, R)) / np.sqrt(L) / s2, "e2m1")
    return {
        "tab_words": p_tab[0],
        "tab_scales": p_tab[1],
        "xT": (n((K, T)) * s).astype(np.float32),
        "wgt2": np.repeat(np.random.uniform(0.5, 2.0, (8, J)), 16, axis=0).astype(np.float32),
        "wa_words": p_wa[0],
        "wa_scales": p_wa[1],
        "wb_words": p_wb[0],
        "wb_scales": p_wb[1],
        "wd": (n((R, N)) / np.sqrt(R) / u).astype(np.float32),
        "b": (0.3 * n(N)).astype(np.float32),
        "offs": striped(np.random.permutation(T)[:J]),
        "offs2": striped8(np.stack([np.random.permutation(T)[:J] for _ in range(8)])),
    }


def reference(tab_words, tab_scales, xT, wgt2, wa_words, wa_scales, wb_words, wb_scales, wd, b, offs, offs2):
    idx = unstriped(offs)
    idx2 = unstriped8(offs2)
    tab_ = unpack_weight(tab_words, tab_scales, "e4m3")[:, idx]
    rows = np.arange(K)
    xg = f64(wgt2)[rows // 4 % 128] * f64(xT)[rows[:, None], idx2[rows % 512 // 64]]
    xT_ = mxq(xg, 0, "e4m3")
    wa_ = unpack_weight(wa_words, wa_scales, "e4m3")
    wb_ = unpack_weight(wb_words, wb_scales, "e2m1")
    ya = wa_.T @ xT_
    yb = wb_.T @ tab_
    h = ya * yb
    h_ = mxq(h, 0, "e4m3")
    wd_ = mxq(f64(wd), 0, "e4m3")
    y = wd_.T @ h_
    return y + f64(b)[:, None]

@@ -1,0 +1,244 @@
+from contextlib import ExitStack
+
+import concourse.mybir as mybir
+
+K, L, R, N, T, J = 512, 512, 512, 512, 2048, 1024
+FLOPS = 2 * J * (K * R + L * R + R * N)
+
+F32 = mybir.dt.float32
+BF16 = mybir.dt.bfloat16
+I32 = mybir.dt.int32
+U32 = mybir.dt.uint32
+U16 = mybir.dt.uint16
+U8 = mybir.dt.uint8
+FP8X4 = mybir.dt.float8_e4m3fn_x4
+FP4X4 = mybir.dt.float4_e2m1fn_x4
+MULT = mybir.AluOpType.mult
+ADD = mybir.AluOpType.add
+IDENTITY = mybir.ActivationFunctionType.Identity
+
+P = 128
+PACK = 4
+LIST_ROWS = 16
+HALF = J // 2
+CHUNK = 256
+UNIT = 128
+X_GROUPS = (512, 256, 256)
+GROUPS = (256, 256, 256, 128, 128)
+
+
+def load_scale_rows(queue, plane, rows):
+    for q in range(4):
+        queue.dma_start(out=plane[32 * q : 32 * q + 4, :].bitcast(I32), in_=rows[4 * q : 4 * q + 4, :].bitcast(I32))
+
+
+def interleave(nc, dst, src):
+    nc.scalar.copy(
+        out=dst.rearrange("p (c i t) -> p c t i", i=4, t=PACK),
+        in_=src.rearrange("p t (c i) -> p c t i", i=4),
+    )
+
+
+def tile_list_htabg_mul_bias_kernel(
+    tc, tab_words, tab_scales, xT, wgt2, wa_words, wa_scales, wb_words, wb_scales, wd, b, offs, offs2, out
+):
+    nc = tc.nc
+    with ExitStack() as ctx:
+        keep = ctx.enter_context(tc.tile_pool(name="keep", bufs=1))
+        psum = ctx.enter_context(tc.psum_pool(name="psum", bufs=4))
+
+        def sb(name, shape, dtype):
+            return keep.tile(shape, dtype, name=name, align_bytes=64)
+
+        offs_sb = keep.tile([P, J // LIST_ROWS], U16, name="offs_sb")
+        offs2_sb = keep.tile([P, J // LIST_ROWS], U16, name="offs2_sb")
+        tab_scale_sb = sb("tab_scale_sb", [P, T], U8)
+        tab_word_sb = sb("tab_word_sb", [P, T], U32)
+        wa_scale_raw = sb("wa_scale_raw", [P, R], U8)
+        wb_scale_raw = sb("wb_scale_raw", [P, R], U8)
+        wa_raw = sb("wa_raw", [P, R], I32)
+        wb_raw = sb("wb_raw", [P, R // 2], I32)
+        xg = [sb("xg%d" % h, [P, PACK + h, HALF], F32) for h in range(2)]
+        wgt_sb = [xg[1][:, 3, :], xg[1][:, 4, :]]
+        x_sb = [sb("x%d" % i, [P, T], F32) for i in range(PACK)]
+        wd_raw = [sb("wd_raw%d" % h, [P, PACK, N // 2], F32) for h in range(2)]
+        bias_sb = sb("bias_sb", [P, 4], F32)
+
+        nc.vector.memset(tab_scale_sb[:].bitcast(I32), 0)
+        nc.vector.memset(wb_scale_raw[:].bitcast(I32), 0)
+        nc.vector.memset(wa_scale_raw[:].bitcast(I32), 0)
+
+        x_planes = xT.rearrange("(p i) t -> i p t", i=PACK)
+        wd_rows = wd.rearrange("(a t e) n -> e a t n", t=PACK, e=4)
+        nc.sync.dma_start(offs_sb[:], offs)
+        load_scale_rows(nc.scalar, tab_scale_sb, tab_scales[0])
+        nc.sync.dma_start(out=tab_word_sb[:].bitcast(I32), in_=tab_words[0].rearrange("p t i -> p (t i)").bitcast(I32))
+        nc.sync.dma_start(out=wb_raw[:], in_=wb_words[0].bitcast(I32))
+        nc.sync.dma_start(offs2_sb[:], offs2)
+        nc.sync.dma_start(out=xg[1][:, 3:5, :], in_=wgt2.rearrange("p (h j) -> p h j", h=2))
+        nc.sync.dma_start(out=x_sb[0][:], in_=x_planes[0])
+        load_scale_rows(nc.scalar, wb_scale_raw, wb_scales[0])
+        nc.sync.dma_start(out=x_sb[1][:], in_=x_planes[1])
+        load_scale_rows(nc.sync, wa_scale_raw, wa_scales[0])
+        nc.sync.dma_start(out=wa_raw[:], in_=wa_words[0].rearrange("p r i -> p (r i)").bitcast(I32))
+        for h in range(2):
+            nc.sync.dma_start(out=x_sb[3 - h][:], in_=x_planes[3 - h])
+            for e in range(4):
+                nc.sync.dma_start(out=wd_raw[h][e:P:4, :, :], in_=wd_rows[e][:, :, h * N // 2 : (h + 1) * N // 2])
+        with nc.allow_non_contiguous_dma(reason="one bias value a partition for each block of 128 output rows"):
+            nc.sync.dma_start(out=bias_sb[:], in_=b.rearrange("(u m) -> m u", u=4))
+
+        v_scales = sb("v_scales", [P, J], U8)
+        v_words = sb("v_words", [P, J], U32)
+        nc.vector.tensor_copy(v_scales[:], tab_scale_sb[:].indirect(offs_sb[:]))
+        nc.vector.tensor_copy(v_words[:], tab_word_sb[:].indirect(offs_sb[:]))
+
+        def deal(name, raw, run):
+            width = raw.shape[1]
+            dealt = sb(name, [P, 4 * width], U8)
+            if run > 1:
+                nc.vector.tensor_copy(
+                    out=dealt[:].bitcast(I32).rearrange("p (t a e) -> p t a e", t=PACK, e=run),
+                    in_=raw.rearrange("p (a t e) -> p t a e", t=PACK, e=run),
+                )
+            else:
+                nc.vector.tensor_copy(
+                    out=dealt[:].bitcast(I32).rearrange("p (t a) -> p t a", t=PACK),
+                    in_=raw.rearrange("p (a t) -> p t a", t=PACK),
+                )
+            return dealt
+
+        wb_codes = deal("wb_codes", wb_raw[:], 2)
+        wb_sc = deal("wb_sc", wb_scale_raw[:].bitcast(I32), 1)
+
+        units = J // UNIT
+        yb_sb = []
+        for c in range(units):
+            bank = psum.tile([P, PACK, UNIT], F32, name="ab_bank")
+            for t in range(PACK):
+                nc.tensor.matmul_mx(
+                    out=bank[:, t, :],
+                    lhsT=wb_codes[:, 2 * P * t : 2 * P * (t + 1)].bitcast(FP4X4),
+                    lhsT_scale=wb_sc[:, P * t : P * (t + 1)],
+                    rhs=v_words[:, c * UNIT : (c + 1) * UNIT].bitcast(FP8X4),
+                    rhs_scale=v_scales[:, c * UNIT : (c + 1) * UNIT],
+                    start=True,
+                    stop=True,
+                )
+            yb = sb("yb%d" % c, [P, UNIT, PACK], F32)
+            nc.scalar.copy(out=yb[:], in_=bank[:].rearrange("p t j -> p j t"))
+            yb_sb.append(yb)
+
+        def pick(i, j0, width):
+            h, c0 = divmod(j0, HALF)
+            nc.vector.tensor_tensor(
+                xg[h][:, i, c0 : c0 + width],
+                x_sb[i][:].indirect(offs2_sb[:, j0 // LIST_ROWS : (j0 + width) // LIST_ROWS]),
+                wgt_sb[h][:, c0 : c0 + width],
+                MULT,
+            )
+
+        for i in range(2):
+            for h in range(2):
+                pick(i, h * HALF, HALF)
+        wa_codes = deal("wa_codes", wa_raw[:], 4)
+        wa_sc = deal("wa_sc", wa_scale_raw[:].bitcast(I32), 1)
+        wd_bf = sb("wd_bf", [P, N * PACK], BF16)
+        interleave(nc, wd_bf[:, 0 : 2 * N], wd_raw[0][:])
+        pick(3, 0, HALF)
+        pick(2, 0, HALF)
+        pick(3, HALF, HALF)
+        pick(2, HALF, CHUNK)
+        pick(2, HALF + CHUNK, CHUNK)
+
+        x_starts = [sum(X_GROUPS[:c]) for c in range(len(X_GROUPS))]
+        x_bf, x_codes, x_sc = [], [], []
+        for c, w in enumerate(X_GROUPS):
+            h, c0 = divmod(x_starts[c], HALF)
+            bf = sb("x_bf%d" % c, [P, w * PACK], BF16)
+            interleave(nc, bf[:], xg[h][:, 0:PACK, c0 : c0 + w])
+            x_bf.append(bf)
+            if c == 0:
+                interleave(nc, wd_bf[:, 2 * N : 4 * N], wd_raw[1][:])
+
+        def quantise_x(c):
+            codes = sb("x_codes%d" % c, [P, X_GROUPS[c]], U32)
+            sc = sb("x_sc%d" % c, [P, X_GROUPS[c]], U8)
+            nc.vector.quantize_mx(out=codes[:].bitcast(FP8X4), scales=sc[:], in_=x_bf[c][:])
+            x_codes.append(codes)
+            x_sc.append(sc)
+
+        wd_codes = sb("wd_codes", [P, N], U32)
+        wd_sc = sb("wd_sc", [P, N], U8)
+        starts = [sum(GROUPS[:g]) for g in range(len(GROUPS))]
+        h_bf = [sb("h_bf%d" % g, [P, w * PACK], BF16) for g, w in enumerate(GROUPS)]
+
+        def first_stage(u):
+            c = max(n for n in range(len(X_GROUPS)) if x_starts[n] <= u * UNIT)
+            c0 = u * UNIT - x_starts[c]
+            bank = psum.tile([P, PACK, UNIT], F32, name="ab_bank")
+            for t in range(PACK):
+                nc.tensor.matmul_mx(
+                    out=bank[:, t, :],
+                    lhsT=wa_codes[:, 4 * P * t : 4 * P * (t + 1)].bitcast(FP8X4),
+                    lhsT_scale=wa_sc[:, P * t : P * (t + 1)],
+                    rhs=x_codes[c][:, c0 : c0 + UNIT].bitcast(FP8X4),
+                    rhs_scale=x_sc[c][:, c0 : c0 + UNIT],
+                    start=True,
+                    stop=True,
+                )
+            g = max(n for n in range(len(GROUPS)) if starts[n] <= u * UNIT)
+            g0 = (u * UNIT - starts[g]) * PACK
+            nc.vector.tensor_tensor(
+                h_bf[g][:, g0 : g0 + UNIT * PACK].rearrange("p (j t) -> p j t", t=PACK),
+                bank[:].rearrange("p t j -> p j t"),
+                yb_sb[u][:],
+                MULT,
+            )
+
+        out_rows = out.rearrange("(u m) j -> m u j", m=P)
+
+        def second_stage(g):
+            w, j0 = GROUPS[g], starts[g]
+            codes = sb("h_codes%d" % g, [P, w], U32)
+            sc = sb("h_sc%d" % g, [P, w], U8)
+            nc.vector.quantize_mx(out=codes[:].bitcast(FP8X4), scales=sc[:], in_=h_bf[g][:])
+            for pair in range(2):
+                bank = psum.tile([P, 2, w], F32, name="y_bank")
+                for s in range(2):
+                    u = 2 * pair + s
+                    nc.tensor.matmul_mx(
+                        out=bank[:, s, :],
+                        lhsT=wd_codes[:, P * u : P * (u + 1)].bitcast(FP8X4),
+                        lhsT_scale=wd_sc[:, P * u : P * (u + 1)],
+                        rhs=codes[:].bitcast(FP8X4),
+                        rhs_scale=sc[:],
+                        start=True,
+                        stop=True,
+                    )
+                res = sb("res%d_%d" % (g, pair), [P, 2, w], F32)
+                for s in range(2):
+                    u = 2 * pair + s
+                    if g == len(GROUPS) - 1:
+                        nc.vector.tensor_scalar(res[:, s, :], bank[:, s, :], bias_sb[:, u : u + 1], None, ADD)
+                    else:
+                        nc.scalar.activation(res[:, s, :], bank[:, s, :], IDENTITY, bias=bias_sb[:, u : u + 1])
+                nc.sync.dma_start(out=out_rows[:, 2 * pair : 2 * pair + 2, j0 : j0 + w], in_=res[:])
+
+        quantise_x(0)
+        first_stage(0)
+        first_stage(1)
+        nc.vector.quantize_mx(out=wd_codes[:].bitcast(FP8X4), scales=wd_sc[:], in_=wd_bf[:])
+        first_stage(2)
+        second_stage(0)
+        quantise_x(1)
+        first_stage(3)
+        first_stage(4)
+        second_stage(1)
+        quantise_x(2)
+        first_stage(5)
+        first_stage(6)
+        second_stage(2)
+        second_stage(3)
+        first_stage(7)
+        second_stage(4)

@@ -23,7 +23,8 @@ LIST_ROWS = 16
 HALF = J // 2
 CHUNK = 256
 UNIT = 128
-X_GROUPS = (512, 256, 256)
+X_GROUPS = (256, 256, 256, 256)
+VECTOR_BANKS = 3
 GROUPS = (256, 256, 256, 128, 128)
 
 
@@ -47,21 +48,21 @@ def tile_list_htabg_mul_bias_kernel(
         keep = ctx.enter_context(tc.tile_pool(name="keep", bufs=1))
         psum = ctx.enter_context(tc.psum_pool(name="psum", bufs=4))
 
-        def sb(name, shape, dtype):
-            return keep.tile(shape, dtype, name=name, align_bytes=64)
+        def sb(name, shape, dtype, tag=""):
+            return keep.tile(shape, dtype, name=name, tag=tag or name, align_bytes=64)
 
         offs_sb = keep.tile([P, J // LIST_ROWS], U16, name="offs_sb")
         offs2_sb = keep.tile([P, J // LIST_ROWS], U16, name="offs2_sb")
         tab_scale_sb = sb("tab_scale_sb", [P, T], U8)
         tab_word_sb = sb("tab_word_sb", [P, T], U32)
         wa_scale_raw = sb("wa_scale_raw", [P, R], U8)
-        wb_scale_raw = sb("wb_scale_raw", [P, R], U8)
+        wb_scale_raw = sb("wb_scale_raw", [P, R], U8, tag="xg")
         wa_raw = sb("wa_raw", [P, R], I32)
         wb_raw = sb("wb_raw", [P, R // 2], I32)
-        xg = [sb("xg%d" % h, [P, PACK + h, HALF], F32) for h in range(2)]
-        wgt_sb = [xg[1][:, 3, :], xg[1][:, 4, :]]
+        wgt_sb = sb("wgt_sb", [P, J], F32)
+        v_scales = sb("v_scales", [P, J], U8)
         x_sb = [sb("x%d" % i, [P, T], F32) for i in range(PACK)]
-        wd_raw = [sb("wd_raw%d" % h, [P, PACK, N // 2], F32) for h in range(2)]
+        wd_raw = sb("wd_raw", [P, PACK, N], F32)
         bias_sb = sb("bias_sb", [P, 4], F32)
 
         nc.vector.memset(tab_scale_sb[:].bitcast(I32), 0)
@@ -70,25 +71,25 @@ def tile_list_htabg_mul_bias_kernel(
 
         x_planes = xT.rearrange("(p i) t -> i p t", i=PACK)
         wd_rows = wd.rearrange("(a t e) n -> e a t n", t=PACK, e=4)
+
         nc.sync.dma_start(offs_sb[:], offs)
-        load_scale_rows(nc.scalar, tab_scale_sb, tab_scales[0])
-        nc.sync.dma_start(out=tab_word_sb[:].bitcast(I32), in_=tab_words[0].rearrange("p t i -> p (t i)").bitcast(I32))
-        nc.sync.dma_start(out=wb_raw[:], in_=wb_words[0].bitcast(I32))
         nc.sync.dma_start(offs2_sb[:], offs2)
-        nc.sync.dma_start(out=xg[1][:, 3:5, :], in_=wgt2.rearrange("p (h j) -> p h j", h=2))
+        nc.sync.dma_start(out=tab_word_sb[:].bitcast(I32), in_=tab_words[0].rearrange("p t i -> p (t i)").bitcast(I32))
+        load_scale_rows(nc.scalar, tab_scale_sb, tab_scales[0])
+        nc.sync.dma_start(out=wb_raw[:], in_=wb_words[0].bitcast(I32))
+        nc.sync.dma_start(out=wgt_sb[:], in_=wgt2)
         nc.sync.dma_start(out=x_sb[0][:], in_=x_planes[0])
-        load_scale_rows(nc.scalar, wb_scale_raw, wb_scales[0])
+        load_scale_rows(nc.sync, wb_scale_raw, wb_scales[0])
         nc.sync.dma_start(out=x_sb[1][:], in_=x_planes[1])
-        load_scale_rows(nc.sync, wa_scale_raw, wa_scales[0])
+        nc.sync.dma_start(out=x_sb[2][:], in_=x_planes[2])
+        for e in range(4):
+            nc.sync.dma_start(out=wd_raw[e:P:4, :, :], in_=wd_rows[e])
+        nc.sync.dma_start(out=x_sb[3][:], in_=x_planes[3])
         nc.sync.dma_start(out=wa_raw[:], in_=wa_words[0].rearrange("p r i -> p (r i)").bitcast(I32))
-        for h in range(2):
-            nc.sync.dma_start(out=x_sb[3 - h][:], in_=x_planes[3 - h])
-            for e in range(4):
-                nc.sync.dma_start(out=wd_raw[h][e:P:4, :, :], in_=wd_rows[e][:, :, h * N // 2 : (h + 1) * N // 2])
+        load_scale_rows(nc.sync, wa_scale_raw, wa_scales[0])
         with nc.allow_non_contiguous_dma(reason="one bias value a partition for each block of 128 output rows"):
             nc.sync.dma_start(out=bias_sb[:], in_=b.rearrange("(u m) -> m u", u=4))
 
-        v_scales = sb("v_scales", [P, J], U8)
         v_words = sb("v_words", [P, J], U32)
         nc.vector.tensor_copy(v_scales[:], tab_scale_sb[:].indirect(offs_sb[:]))
         nc.vector.tensor_copy(v_words[:], tab_word_sb[:].indirect(offs_sb[:]))
@@ -129,37 +130,33 @@ def tile_list_htabg_mul_bias_kernel(
             nc.scalar.copy(out=yb[:], in_=bank[:].rearrange("p t j -> p j t"))
             yb_sb.append(yb)
 
+        xg = sb("xg", [P, PACK, J], F32)
+
         def pick(i, j0, width):
-            h, c0 = divmod(j0, HALF)
             nc.vector.tensor_tensor(
-                xg[h][:, i, c0 : c0 + width],
+                xg[:, i, j0 : j0 + width],
                 x_sb[i][:].indirect(offs2_sb[:, j0 // LIST_ROWS : (j0 + width) // LIST_ROWS]),
-                wgt_sb[h][:, c0 : c0 + width],
+                wgt_sb[:, j0 : j0 + width],
                 MULT,
             )
 
-        for i in range(2):
-            for h in range(2):
-                pick(i, h * HALF, HALF)
+        for i in range(PACK - 1):
+            pick(i, 0, J)
+        wd_bf = sb("wd_bf", [P, N * PACK], BF16)
+        interleave(nc, wd_bf[:], wd_raw[:])
+        wd_codes = sb("wd_codes", [P, N], U32, tag="wgt_sb")
+        wd_sc = sb("wd_sc", [P, N], U8)
+        for c in range(J // CHUNK):
+            pick(PACK - 1, c * CHUNK, CHUNK)
         wa_codes = deal("wa_codes", wa_raw[:], 4)
         wa_sc = deal("wa_sc", wa_scale_raw[:].bitcast(I32), 1)
-        wd_bf = sb("wd_bf", [P, N * PACK], BF16)
-        interleave(nc, wd_bf[:, 0 : 2 * N], wd_raw[0][:])
-        pick(3, 0, HALF)
-        pick(2, 0, HALF)
-        pick(3, HALF, HALF)
-        pick(2, HALF, CHUNK)
-        pick(2, HALF + CHUNK, CHUNK)
 
         x_starts = [sum(X_GROUPS[:c]) for c in range(len(X_GROUPS))]
         x_bf, x_codes, x_sc = [], [], []
         for c, w in enumerate(X_GROUPS):
-            h, c0 = divmod(x_starts[c], HALF)
             bf = sb("x_bf%d" % c, [P, w * PACK], BF16)
-            interleave(nc, bf[:], xg[h][:, 0:PACK, c0 : c0 + w])
+            interleave(nc, bf[:], xg[:, :, x_starts[c] : x_starts[c] + w])
             x_bf.append(bf)
-            if c == 0:
-                interleave(nc, wd_bf[:, 2 * N : 4 * N], wd_raw[1][:])
 
         def quantise_x(c):
             codes = sb("x_codes%d" % c, [P, X_GROUPS[c]], U32)
@@ -168,8 +165,6 @@ def tile_list_htabg_mul_bias_kernel(
             x_codes.append(codes)
             x_sc.append(sc)
 
-        wd_codes = sb("wd_codes", [P, N], U32)
-        wd_sc = sb("wd_sc", [P, N], U8)
         starts = [sum(GROUPS[:g]) for g in range(len(GROUPS))]
         h_bf = [sb("h_bf%d" % g, [P, w * PACK], BF16) for g, w in enumerate(GROUPS)]
 
@@ -203,10 +198,10 @@ def tile_list_htabg_mul_bias_kernel(
             codes = sb("h_codes%d" % g, [P, w], U32)
             sc = sb("h_sc%d" % g, [P, w], U8)
             nc.vector.quantize_mx(out=codes[:].bitcast(FP8X4), scales=sc[:], in_=h_bf[g][:])
-            for pair in range(2):
+            for u0 in (0, 2):
                 bank = psum.tile([P, 2, w], F32, name="y_bank")
                 for s in range(2):
-                    u = 2 * pair + s
+                    u = u0 + s
                     nc.tensor.matmul_mx(
                         out=bank[:, s, :],
                         lhsT=wd_codes[:, P * u : P * (u + 1)].bitcast(FP8X4),
@@ -216,29 +211,31 @@ def tile_list_htabg_mul_bias_kernel(
                         start=True,
                         stop=True,
                     )
-                res = sb("res%d_%d" % (g, pair), [P, 2, w], F32)
-                for s in range(2):
-                    u = 2 * pair + s
-                    if g == len(GROUPS) - 1:
-                        nc.vector.tensor_scalar(res[:, s, :], bank[:, s, :], bias_sb[:, u : u + 1], None, ADD)
-                    else:
+                res = sb("res%d_%d" % (g, u0), [P, 2, w], F32)
+                if 2 * g + u0 // 2 >= 2 * len(GROUPS) - VECTOR_BANKS:
+                    spread = bias_sb[:, u0 : u0 + 2].unsqueeze(2).to_broadcast([P, 2, w])
+                    nc.vector.tensor_tensor(res[:], bank[:], spread, ADD)
+                else:
+                    for s in range(2):
+                        u = u0 + s
                         nc.scalar.activation(res[:, s, :], bank[:, s, :], IDENTITY, bias=bias_sb[:, u : u + 1])
-                nc.sync.dma_start(out=out_rows[:, 2 * pair : 2 * pair + 2, j0 : j0 + w], in_=res[:])
+                nc.sync.dma_start(out=out_rows[:, u0 : u0 + 2, j0 : j0 + w], in_=res[:])
 
         quantise_x(0)
+        nc.vector.quantize_mx(out=wd_codes[:].bitcast(FP8X4), scales=wd_sc[:], in_=wd_bf[:])
+        quantise_x(1)
         first_stage(0)
         first_stage(1)
-        nc.vector.quantize_mx(out=wd_codes[:].bitcast(FP8X4), scales=wd_sc[:], in_=wd_bf[:])
+        quantise_x(2)
         first_stage(2)
         second_stage(0)
-        quantise_x(1)
         first_stage(3)
+        quantise_x(3)
         first_stage(4)
         second_stage(1)
-        quantise_x(2)
         first_stage(5)
         first_stage(6)
         second_stage(2)
-        second_stage(3)
         first_stage(7)
+        second_stage(3)
         second_stage(4)

@@ -75,7 +75,7 @@ def tile_list_htabg_mul_bias_kernel(
         nc.sync.dma_start(offs_sb[:], offs)
         nc.sync.dma_start(offs2_sb[:], offs2)
         nc.sync.dma_start(out=tab_word_sb[:].bitcast(I32), in_=tab_words[0].rearrange("p t i -> p (t i)").bitcast(I32))
-        load_scale_rows(nc.scalar, tab_scale_sb, tab_scales[0])
+        load_scale_rows(nc.sync, tab_scale_sb, tab_scales[0])
         nc.sync.dma_start(out=wb_raw[:], in_=wb_words[0].bitcast(I32))
         nc.sync.dma_start(out=wgt_sb[:], in_=wgt2)
         nc.sync.dma_start(out=x_sb[0][:], in_=x_planes[0])
@@ -91,8 +91,8 @@ def tile_list_htabg_mul_bias_kernel(
             nc.sync.dma_start(out=bias_sb[:], in_=b.rearrange("(u m) -> m u", u=4))
 
         v_words = sb("v_words", [P, J], U32)
-        nc.vector.tensor_copy(v_scales[:], tab_scale_sb[:].indirect(offs_sb[:]))
         nc.vector.tensor_copy(v_words[:], tab_word_sb[:].indirect(offs_sb[:]))
+        nc.vector.tensor_copy(v_scales[:], tab_scale_sb[:].indirect(offs_sb[:]))
 
         def deal(name, raw, run):
             width = raw.shape[1]

@@ -1,6 +1,7 @@
 from contextlib import ExitStack
 
 import concourse.mybir as mybir
+from concourse.masks import make_identity
 
 K, L, R, N, T, J = 512, 512, 512, 512, 2048, 1024
 FLOPS = 2 * J * (K * R + L * R + R * N)
@@ -20,17 +21,16 @@ IDENTITY = mybir.ActivationFunctionType.Identity
 P = 128
 PACK = 4
 LIST_ROWS = 16
-HALF = J // 2
+HEADS = 8
+RUN = 8
 CHUNK = 256
 UNIT = 128
-X_GROUPS = (256, 256, 256, 256)
+EARLY_CHUNKS = 3
 VECTOR_BANKS = 3
 GROUPS = (256, 256, 256, 128, 128)
-
-
-def load_scale_rows(queue, plane, rows):
-    for q in range(4):
-        queue.dma_start(out=plane[32 * q : 32 * q + 4, :].bitcast(I32), in_=rows[4 * q : 4 * q + 4, :].bitcast(I32))
+TAB_ROW0 = 112
+W_ROW0 = 96
+BIAS_ROW0 = 124
 
 
 def interleave(nc, dst, src):
@@ -51,76 +51,104 @@ def tile_list_htabg_mul_bias_kernel(
         def sb(name, shape, dtype, tag=""):
             return keep.tile(shape, dtype, name=name, tag=tag or name, align_bytes=64)
 
+        def move_scale_rows(plane, rows, row0):
+            for q in range(4):
+                nc.sync.dma_start(
+                    out=plane[32 * q : 32 * q + 4, :].bitcast(I32),
+                    in_=rows[row0 + 4 * q : row0 + 4 * q + 4, :].bitcast(I32),
+                )
+
         offs_sb = keep.tile([P, J // LIST_ROWS], U16, name="offs_sb")
         offs2_sb = keep.tile([P, J // LIST_ROWS], U16, name="offs2_sb")
         tab_scale_sb = sb("tab_scale_sb", [P, T], U8)
-        tab_word_sb = sb("tab_word_sb", [P, T], U32)
-        wa_scale_raw = sb("wa_scale_raw", [P, R], U8)
-        wb_scale_raw = sb("wb_scale_raw", [P, R], U8, tag="xg")
-        wa_raw = sb("wa_raw", [P, R], I32)
+        w_scale_raw = sb("w_scale_raw", [P, 2 * R], U8)
+        rows_sb = sb("rows_sb", [P, P], F32)
+        ident = sb("ident", [P, P], F32)
+        tab_word_sb = sb("tab_word_sb", [P, T], U32, tag="big_a")
         wb_raw = sb("wb_raw", [P, R // 2], I32)
-        wgt_sb = sb("wgt_sb", [P, J], F32)
-        v_scales = sb("v_scales", [P, J], U8)
-        x_sb = [sb("x%d" % i, [P, T], F32) for i in range(PACK)]
-        wd_raw = sb("wd_raw", [P, PACK, N], F32)
-        bias_sb = sb("bias_sb", [P, 4], F32)
 
-        nc.vector.memset(tab_scale_sb[:].bitcast(I32), 0)
-        nc.vector.memset(wb_scale_raw[:].bitcast(I32), 0)
-        nc.vector.memset(wa_scale_raw[:].bitcast(I32), 0)
+        make_identity(nc, ident[:])
+        nc.vector.memset(tab_scale_sb[0:96, :].bitcast(I32), 0)
+        nc.vector.memset(tab_scale_sb[96:TAB_ROW0, :].bitcast(I32), 0)
+        nc.vector.memset(rows_sb[64:96, :], 0.0)
+        nc.vector.memset(rows_sb[96:BIAS_ROW0, :], 0.0)
 
         x_planes = xT.rearrange("(p i) t -> i p t", i=PACK)
-        wd_rows = wd.rearrange("(a t e) n -> e a t n", t=PACK, e=4)
+        wd_rows = wd.rearrange("(a t e) n -> t a e n", t=PACK, e=RUN)
+        wgt_rows = wgt2.rearrange("(g s) (c k) -> s g c k", s=LIST_ROWS, k=P)[0]
 
+        w_rows = w_scale_raw[W_ROW0 : W_ROW0 + 16, :].bitcast(I32)
+        nc.scalar.dma_start(out=w_rows[:, 0 : R // 4], in_=wb_scales[0].bitcast(I32))
+        nc.scalar.dma_start(out=w_rows[:, R // 4 : R // 2], in_=wa_scales[0].bitcast(I32))
         nc.sync.dma_start(offs_sb[:], offs)
-        nc.sync.dma_start(offs2_sb[:], offs2)
+        nc.sync.dma_start(out=tab_scale_sb[TAB_ROW0:P, :].bitcast(I32), in_=tab_scales[0].bitcast(I32))
+        nc.sync.dma_start(out=rows_sb[0:64, :], in_=wgt_rows)
+        nc.sync.dma_start(out=rows_sb[BIAS_ROW0:P, :], in_=b.rearrange("(u m) -> u m", m=P))
         nc.sync.dma_start(out=tab_word_sb[:].bitcast(I32), in_=tab_words[0].rearrange("p t i -> p (t i)").bitcast(I32))
-        load_scale_rows(nc.sync, tab_scale_sb, tab_scales[0])
         nc.sync.dma_start(out=wb_raw[:], in_=wb_words[0].bitcast(I32))
-        nc.sync.dma_start(out=wgt_sb[:], in_=wgt2)
-        nc.sync.dma_start(out=x_sb[0][:], in_=x_planes[0])
-        load_scale_rows(nc.sync, wb_scale_raw, wb_scales[0])
-        nc.sync.dma_start(out=x_sb[1][:], in_=x_planes[1])
-        nc.sync.dma_start(out=x_sb[2][:], in_=x_planes[2])
-        for e in range(4):
-            nc.sync.dma_start(out=wd_raw[e:P:4, :, :], in_=wd_rows[e])
-        nc.sync.dma_start(out=x_sb[3][:], in_=x_planes[3])
-        nc.sync.dma_start(out=wa_raw[:], in_=wa_words[0].rearrange("p r i -> p (r i)").bitcast(I32))
-        load_scale_rows(nc.sync, wa_scale_raw, wa_scales[0])
-        with nc.allow_non_contiguous_dma(reason="one bias value a partition for each block of 128 output rows"):
-            nc.sync.dma_start(out=bias_sb[:], in_=b.rearrange("(u m) -> m u", u=4))
 
-        v_words = sb("v_words", [P, J], U32)
-        nc.vector.tensor_copy(v_words[:], tab_word_sb[:].indirect(offs_sb[:]))
-        nc.vector.tensor_copy(v_scales[:], tab_scale_sb[:].indirect(offs_sb[:]))
+        w_scale_dealt = sb("w_scale_dealt", [P, 2 * R], U8)
+        nc.vector.tensor_copy(
+            out=w_scale_dealt[W_ROW0 : W_ROW0 + 16, :].bitcast(I32).rearrange("p (w t a e) -> p w t a e", w=2, t=PACK, e=RUN // 4),
+            in_=w_rows.rearrange("p (w a t e) -> p w t a e", w=2, t=PACK, e=RUN // 4),
+        )
+        w_sc = sb("w_sc", [P, 2 * R], U8)
+        move_scale_rows(w_sc, w_scale_dealt, W_ROW0)
+
+        x_sb = [sb("x0", [P, T], F32, tag="big_b"), sb("x1", [P, T], F32, tag="big_c")]
+        nc.sync.dma_start(out=x_sb[0][:], in_=x_planes[0])
+        nc.sync.dma_start(offs2_sb[:], offs2)
+
+        v_scale_rows = sb("v_scale_rows", [P, J], U8)
+        nc.vector.tensor_copy(v_scale_rows[:], tab_scale_sb[:].indirect(offs_sb[:]))
+        v_scales = sb("v_scales", [P, J], U8)
+        move_scale_rows(v_scales, v_scale_rows, TAB_ROW0)
+        nc.sync.dma_start(out=x_sb[1][:], in_=x_planes[1])
 
         def deal(name, raw, run):
             width = raw.shape[1]
             dealt = sb(name, [P, 4 * width], U8)
-            if run > 1:
-                nc.vector.tensor_copy(
-                    out=dealt[:].bitcast(I32).rearrange("p (t a e) -> p t a e", t=PACK, e=run),
-                    in_=raw.rearrange("p (a t e) -> p t a e", t=PACK, e=run),
-                )
-            else:
-                nc.vector.tensor_copy(
-                    out=dealt[:].bitcast(I32).rearrange("p (t a) -> p t a", t=PACK),
-                    in_=raw.rearrange("p (a t) -> p t a", t=PACK),
-                )
+            nc.vector.tensor_copy(
+                out=dealt[:].bitcast(I32).rearrange("p (t a e) -> p t a e", t=PACK, e=run),
+                in_=raw.rearrange("p (a t e) -> p t a e", t=PACK, e=run),
+            )
             return dealt
 
-        wb_codes = deal("wb_codes", wb_raw[:], 2)
-        wb_sc = deal("wb_sc", wb_scale_raw[:].bitcast(I32), 1)
+        wb_codes = deal("wb_codes", wb_raw[:], RUN // 2)
+        v_words = sb("v_words", [P, J], U32)
+        nc.vector.tensor_copy(v_words[:], tab_word_sb[:].indirect(offs_sb[:]))
+
+        turned = psum.tile([P, P], F32, name="turned", tag="y_bank", bufs=5)
+        nc.tensor.transpose(turned[:], rows_sb[:], ident[:])
+        spread = sb("spread", [P, J // P, P], F32)
+        wgt_sb = sb("wgt_sb", [P, J], F32)
+        bias_sb = sb("bias_sb", [P, 4], F32)
+        by_chunk = turned[:, 0:64].rearrange("p (g c) -> p c g", g=HEADS)
+        for h in range(2):
+            cs = slice(4 * h, 4 * h + 4)
+            nc.scalar.copy(
+                out=spread[:, cs, :].rearrange("p c (g s) -> p c g s", g=HEADS),
+                in_=by_chunk[:, cs, :].unsqueeze(3).to_broadcast([P, 4, HEADS, LIST_ROWS]),
+            )
+        nc.scalar.copy(out=bias_sb[:], in_=turned[:, BIAS_ROW0:P])
+        for h in range(2):
+            back = psum.tile([P, 4, P], F32, name="back", tag="y_bank", bufs=5)
+            for c in range(4):
+                nc.tensor.transpose(back[:, c, :], spread[:, 4 * h + c, :], ident[:])
+            nc.scalar.copy(out=wgt_sb[:, 512 * h : 512 * (h + 1)], in_=back[:].rearrange("p c k -> p (c k)"))
+
+        x_sb.append(sb("x2", [P, T], F32, tag="big_a"))
+        nc.sync.dma_start(out=x_sb[2][:], in_=x_planes[2])
 
         units = J // UNIT
         yb_sb = []
         for c in range(units):
-            bank = psum.tile([P, PACK, UNIT], F32, name="ab_bank")
+            bank = psum.tile([P, PACK, UNIT], F32, name="ab_bank", bufs=3)
             for t in range(PACK):
                 nc.tensor.matmul_mx(
                     out=bank[:, t, :],
                     lhsT=wb_codes[:, 2 * P * t : 2 * P * (t + 1)].bitcast(FP4X4),
-                    lhsT_scale=wb_sc[:, P * t : P * (t + 1)],
+                    lhsT_scale=w_sc[:, P * t : P * (t + 1)],
                     rhs=v_words[:, c * UNIT : (c + 1) * UNIT].bitcast(FP8X4),
                     rhs_scale=v_scales[:, c * UNIT : (c + 1) * UNIT],
                     start=True,
@@ -140,43 +168,59 @@ def tile_list_htabg_mul_bias_kernel(
                 MULT,
             )
 
-        for i in range(PACK - 1):
-            pick(i, 0, J)
-        wd_bf = sb("wd_bf", [P, N * PACK], BF16)
-        interleave(nc, wd_bf[:], wd_raw[:])
-        wd_codes = sb("wd_codes", [P, N], U32, tag="wgt_sb")
-        wd_sc = sb("wd_sc", [P, N], U8)
-        for c in range(J // CHUNK):
-            pick(PACK - 1, c * CHUNK, CHUNK)
-        wa_codes = deal("wa_codes", wa_raw[:], 4)
-        wa_sc = deal("wa_sc", wa_scale_raw[:].bitcast(I32), 1)
+        chunks = J // CHUNK
+        x_bf = [sb("x_bf%d" % c, [P, CHUNK * PACK], BF16) for c in range(chunks)]
 
-        x_starts = [sum(X_GROUPS[:c]) for c in range(len(X_GROUPS))]
-        x_bf, x_codes, x_sc = [], [], []
-        for c, w in enumerate(X_GROUPS):
-            bf = sb("x_bf%d" % c, [P, w * PACK], BF16)
-            interleave(nc, bf[:], xg[:, :, x_starts[c] : x_starts[c] + w])
-            x_bf.append(bf)
+        def round_pair(c, i0):
+            nc.scalar.copy(
+                out=x_bf[c][:].rearrange("p (j t) -> p j t", t=PACK)[:, :, i0 : i0 + 2],
+                in_=xg[:, i0 : i0 + 2, c * CHUNK : (c + 1) * CHUNK].rearrange("p t j -> p j t"),
+            )
+
+        pick(0, 0, J)
+        x_sb.append(sb("x3", [P, T], F32, tag="big_b"))
+        nc.sync.dma_start(out=x_sb[3][:], in_=x_planes[3])
+        pick(1, 0, J)
+        wa_raw = sb("wa_raw", [P, R], I32, tag="wb_raw")
+        wd_raw = sb("wd_raw", [P, PACK, N], F32, tag="big_c")
+        nc.sync.dma_start(out=wa_raw[:], in_=wa_words[0].rearrange("p r i -> p (r i)").bitcast(I32))
+        for t in range(PACK):
+            nc.sync.dma_start(out=wd_raw[:, t, :], in_=wd_rows[t])
+        for c in range(EARLY_CHUNKS):
+            round_pair(c, 0)
+        pick(2, 0, J)
+
+        x_codes, x_sc = [], []
 
         def quantise_x(c):
-            codes = sb("x_codes%d" % c, [P, X_GROUPS[c]], U32)
-            sc = sb("x_sc%d" % c, [P, X_GROUPS[c]], U8)
+            codes = sb("x_codes%d" % c, [P, CHUNK], U32)
+            sc = sb("x_sc%d" % c, [P, CHUNK], U8)
             nc.vector.quantize_mx(out=codes[:].bitcast(FP8X4), scales=sc[:], in_=x_bf[c][:])
             x_codes.append(codes)
             x_sc.append(sc)
+
+        wd_codes, wd_sc = [], []
+
+        def quantise_wd(h):
+            bf = sb("wd_bf%d" % h, [P, N // 2 * PACK], BF16)
+            interleave(nc, bf[:], wd_raw[:, :, h * N // 2 : (h + 1) * N // 2])
+            codes = sb("wd_codes%d" % h, [P, N // 2], U32)
+            sc = sb("wd_sc%d" % h, [P, N // 2], U8)
+            nc.vector.quantize_mx(out=codes[:].bitcast(FP8X4), scales=sc[:], in_=bf[:])
+            wd_codes.append(codes)
+            wd_sc.append(sc)
 
         starts = [sum(GROUPS[:g]) for g in range(len(GROUPS))]
         h_bf = [sb("h_bf%d" % g, [P, w * PACK], BF16) for g, w in enumerate(GROUPS)]
 
         def first_stage(u):
-            c = max(n for n in range(len(X_GROUPS)) if x_starts[n] <= u * UNIT)
-            c0 = u * UNIT - x_starts[c]
-            bank = psum.tile([P, PACK, UNIT], F32, name="ab_bank")
+            c, c0 = divmod(u * UNIT, CHUNK)
+            bank = psum.tile([P, PACK, UNIT], F32, name="ab_bank", bufs=3)
             for t in range(PACK):
                 nc.tensor.matmul_mx(
                     out=bank[:, t, :],
                     lhsT=wa_codes[:, 4 * P * t : 4 * P * (t + 1)].bitcast(FP8X4),
-                    lhsT_scale=wa_sc[:, P * t : P * (t + 1)],
+                    lhsT_scale=w_sc[:, R + P * t : R + P * (t + 1)],
                     rhs=x_codes[c][:, c0 : c0 + UNIT].bitcast(FP8X4),
                     rhs_scale=x_sc[c][:, c0 : c0 + UNIT],
                     start=True,
@@ -192,50 +236,73 @@ def tile_list_htabg_mul_bias_kernel(
             )
 
         out_rows = out.rearrange("(u m) j -> m u j", m=P)
+        h_codes, h_sc = [], []
 
-        def second_stage(g):
-            w, j0 = GROUPS[g], starts[g]
+        def quantise_h(g):
+            w = GROUPS[g]
             codes = sb("h_codes%d" % g, [P, w], U32)
             sc = sb("h_sc%d" % g, [P, w], U8)
             nc.vector.quantize_mx(out=codes[:].bitcast(FP8X4), scales=sc[:], in_=h_bf[g][:])
-            for u0 in (0, 2):
-                bank = psum.tile([P, 2, w], F32, name="y_bank")
+            h_codes.append(codes)
+            h_sc.append(sc)
+
+        def second_stage(g):
+            w, j0 = GROUPS[g], starts[g]
+            for h in range(2):
+                bank = psum.tile([P, 2, w], F32, name="y_bank", bufs=5)
                 for s in range(2):
-                    u = u0 + s
                     nc.tensor.matmul_mx(
                         out=bank[:, s, :],
-                        lhsT=wd_codes[:, P * u : P * (u + 1)].bitcast(FP8X4),
-                        lhsT_scale=wd_sc[:, P * u : P * (u + 1)],
-                        rhs=codes[:].bitcast(FP8X4),
-                        rhs_scale=sc[:],
+                        lhsT=wd_codes[h][:, P * s : P * (s + 1)].bitcast(FP8X4),
+                        lhsT_scale=wd_sc[h][:, P * s : P * (s + 1)],
+                        rhs=h_codes[g][:].bitcast(FP8X4),
+                        rhs_scale=h_sc[g][:],
                         start=True,
                         stop=True,
                     )
-                res = sb("res%d_%d" % (g, u0), [P, 2, w], F32)
-                if 2 * g + u0 // 2 >= 2 * len(GROUPS) - VECTOR_BANKS:
-                    spread = bias_sb[:, u0 : u0 + 2].unsqueeze(2).to_broadcast([P, 2, w])
-                    nc.vector.tensor_tensor(res[:], bank[:], spread, ADD)
+                res = sb("res%d_%d" % (g, h), [P, 2, w], F32)
+                if h == 1 and g >= len(GROUPS) - VECTOR_BANKS:
+                    wide = bias_sb[:, 2 * h : 2 * h + 2].unsqueeze(2).to_broadcast([P, 2, w])
+                    nc.vector.tensor_tensor(res[:], bank[:], wide, ADD)
                 else:
                     for s in range(2):
-                        u = u0 + s
+                        u = 2 * h + s
                         nc.scalar.activation(res[:, s, :], bank[:, s, :], IDENTITY, bias=bias_sb[:, u : u + 1])
-                nc.sync.dma_start(out=out_rows[:, u0 : u0 + 2, j0 : j0 + w], in_=res[:])
+                nc.sync.dma_start(out=out_rows[:, 2 * h : 2 * h + 2, j0 : j0 + w], in_=res[:])
 
+        def last_pick(c):
+            pick(PACK - 1, c * CHUNK, CHUNK)
+            if c < EARLY_CHUNKS:
+                round_pair(c, 2)
+            else:
+                interleave(nc, x_bf[c][:], xg[:, :, c * CHUNK : (c + 1) * CHUNK])
+
+        last_pick(0)
+        last_pick(1)
+        wa_codes = deal("wa_codes", wa_raw[:], RUN)
+        last_pick(2)
         quantise_x(0)
-        nc.vector.quantize_mx(out=wd_codes[:].bitcast(FP8X4), scales=wd_sc[:], in_=wd_bf[:])
+        last_pick(3)
         quantise_x(1)
         first_stage(0)
         first_stage(1)
         quantise_x(2)
         first_stage(2)
-        second_stage(0)
+        quantise_h(0)
+        quantise_wd(0)
         first_stage(3)
         quantise_x(3)
+        quantise_wd(1)
+        second_stage(0)
         first_stage(4)
+        quantise_h(1)
         second_stage(1)
         first_stage(5)
         first_stage(6)
+        quantise_h(2)
         second_stage(2)
         first_stage(7)
+        quantise_h(3)
         second_stage(3)
+        quantise_h(4)
         second_stage(4)

@@ -25,12 +25,12 @@ HEADS = 8
 RUN = 8
 CHUNK = 256
 UNIT = 128
+WIDE = 512
 EARLY_CHUNKS = 3
 VECTOR_BANKS = 3
 GROUPS = (256, 256, 256, 128, 128)
 TAB_ROW0 = 112
 W_ROW0 = 96
-BIAS_ROW0 = 124
 
 
 def interleave(nc, dst, src):
@@ -70,20 +70,18 @@ def tile_list_htabg_mul_bias_kernel(
         make_identity(nc, ident[:])
         nc.vector.memset(tab_scale_sb[0:96, :].bitcast(I32), 0)
         nc.vector.memset(tab_scale_sb[96:TAB_ROW0, :].bitcast(I32), 0)
-        nc.vector.memset(rows_sb[64:96, :], 0.0)
-        nc.vector.memset(rows_sb[96:BIAS_ROW0, :], 0.0)
+        nc.vector.memset(rows_sb[64:P, :], 0.0)
 
         x_planes = xT.rearrange("(p i) t -> i p t", i=PACK)
         wd_rows = wd.rearrange("(a t e) n -> t a e n", t=PACK, e=RUN)
         wgt_rows = wgt2.rearrange("(g s) (c k) -> s g c k", s=LIST_ROWS, k=P)[0]
 
         w_rows = w_scale_raw[W_ROW0 : W_ROW0 + 16, :].bitcast(I32)
-        nc.scalar.dma_start(out=w_rows[:, 0 : R // 4], in_=wb_scales[0].bitcast(I32))
+        nc.sync.dma_start(out=w_rows[:, 0 : R // 4], in_=wb_scales[0].bitcast(I32))
         nc.scalar.dma_start(out=w_rows[:, R // 4 : R // 2], in_=wa_scales[0].bitcast(I32))
         nc.sync.dma_start(offs_sb[:], offs)
-        nc.sync.dma_start(out=tab_scale_sb[TAB_ROW0:P, :].bitcast(I32), in_=tab_scales[0].bitcast(I32))
+        nc.scalar.dma_start(out=tab_scale_sb[TAB_ROW0:P, :].bitcast(I32), in_=tab_scales[0].bitcast(I32))
         nc.sync.dma_start(out=rows_sb[0:64, :], in_=wgt_rows)
-        nc.sync.dma_start(out=rows_sb[BIAS_ROW0:P, :], in_=b.rearrange("(u m) -> u m", m=P))
         nc.sync.dma_start(out=tab_word_sb[:].bitcast(I32), in_=tab_words[0].rearrange("p t i -> p (t i)").bitcast(I32))
         nc.sync.dma_start(out=wb_raw[:], in_=wb_words[0].bitcast(I32))
 
@@ -105,16 +103,16 @@ def tile_list_htabg_mul_bias_kernel(
         move_scale_rows(v_scales, v_scale_rows, TAB_ROW0)
         nc.sync.dma_start(out=x_sb[1][:], in_=x_planes[1])
 
-        def deal(name, raw, run):
+        def deal(engine, name, raw, run):
             width = raw.shape[1]
             dealt = sb(name, [P, 4 * width], U8)
-            nc.vector.tensor_copy(
+            engine.tensor_copy(
                 out=dealt[:].bitcast(I32).rearrange("p (t a e) -> p t a e", t=PACK, e=run),
                 in_=raw.rearrange("p (a t e) -> p t a e", t=PACK, e=run),
             )
             return dealt
 
-        wb_codes = deal("wb_codes", wb_raw[:], RUN // 2)
+        wb_codes = deal(nc.gpsimd, "wb_codes", wb_raw[:], RUN // 2)
         v_words = sb("v_words", [P, J], U32)
         nc.vector.tensor_copy(v_words[:], tab_word_sb[:].indirect(offs_sb[:]))
 
@@ -122,7 +120,6 @@ def tile_list_htabg_mul_bias_kernel(
         nc.tensor.transpose(turned[:], rows_sb[:], ident[:])
         spread = sb("spread", [P, J // P, P], F32)
         wgt_sb = sb("wgt_sb", [P, J], F32)
-        bias_sb = sb("bias_sb", [P, 4], F32)
         by_chunk = turned[:, 0:64].rearrange("p (g c) -> p c g", g=HEADS)
         for h in range(2):
             cs = slice(4 * h, 4 * h + 4)
@@ -130,7 +127,6 @@ def tile_list_htabg_mul_bias_kernel(
                 out=spread[:, cs, :].rearrange("p c (g s) -> p c g s", g=HEADS),
                 in_=by_chunk[:, cs, :].unsqueeze(3).to_broadcast([P, 4, HEADS, LIST_ROWS]),
             )
-        nc.scalar.copy(out=bias_sb[:], in_=turned[:, BIAS_ROW0:P])
         for h in range(2):
             back = psum.tile([P, 4, P], F32, name="back", tag="y_bank", bufs=5)
             for c in range(4):
@@ -140,22 +136,22 @@ def tile_list_htabg_mul_bias_kernel(
         x_sb.append(sb("x2", [P, T], F32, tag="big_a"))
         nc.sync.dma_start(out=x_sb[2][:], in_=x_planes[2])
 
-        units = J // UNIT
         yb_sb = []
-        for c in range(units):
-            bank = psum.tile([P, PACK, UNIT], F32, name="ab_bank", bufs=3)
+        for h in range(J // WIDE):
+            cols = slice(h * WIDE, (h + 1) * WIDE)
+            yb = sb("yb%d" % h, [P, PACK, WIDE], F32)
             for t in range(PACK):
+                bank = psum.tile([P, WIDE], F32, name="ab_bank", bufs=3)
                 nc.tensor.matmul_mx(
-                    out=bank[:, t, :],
+                    out=bank[:],
                     lhsT=wb_codes[:, 2 * P * t : 2 * P * (t + 1)].bitcast(FP4X4),
                     lhsT_scale=w_sc[:, P * t : P * (t + 1)],
-                    rhs=v_words[:, c * UNIT : (c + 1) * UNIT].bitcast(FP8X4),
-                    rhs_scale=v_scales[:, c * UNIT : (c + 1) * UNIT],
+                    rhs=v_words[:, cols].bitcast(FP8X4),
+                    rhs_scale=v_scales[:, cols],
                     start=True,
                     stop=True,
                 )
-            yb = sb("yb%d" % c, [P, UNIT, PACK], F32)
-            nc.scalar.copy(out=yb[:], in_=bank[:].rearrange("p t j -> p j t"))
+                nc.scalar.copy(out=yb[:, t, :], in_=bank[:])
             yb_sb.append(yb)
 
         xg = sb("xg", [P, PACK, J], F32)
@@ -189,6 +185,9 @@ def tile_list_htabg_mul_bias_kernel(
         for c in range(EARLY_CHUNKS):
             round_pair(c, 0)
         pick(2, 0, J)
+        bias_sb = sb("bias_sb", [P, 4], F32, tag="big_a")
+        with nc.allow_non_contiguous_dma(reason="one bias value a partition for each block of 128 output rows"):
+            nc.sync.dma_start(out=bias_sb[:], in_=b.rearrange("(u m) -> m u", u=4))
 
         x_codes, x_sc = [], []
 
@@ -215,6 +214,7 @@ def tile_list_htabg_mul_bias_kernel(
 
         def first_stage(u):
             c, c0 = divmod(u * UNIT, CHUNK)
+            h, b0 = divmod(u * UNIT, WIDE)
             bank = psum.tile([P, PACK, UNIT], F32, name="ab_bank", bufs=3)
             for t in range(PACK):
                 nc.tensor.matmul_mx(
@@ -229,9 +229,9 @@ def tile_list_htabg_mul_bias_kernel(
             g = max(n for n in range(len(GROUPS)) if starts[n] <= u * UNIT)
             g0 = (u * UNIT - starts[g]) * PACK
             nc.vector.tensor_tensor(
-                h_bf[g][:, g0 : g0 + UNIT * PACK].rearrange("p (j t) -> p j t", t=PACK),
-                bank[:].rearrange("p t j -> p j t"),
-                yb_sb[u][:],
+                h_bf[g][:, g0 : g0 + UNIT * PACK].rearrange("p (c i t) -> p c t i", i=4, t=PACK),
+                bank[:].rearrange("p t (c i) -> p c t i", i=4),
+                yb_sb[h][:, :, b0 : b0 + UNIT].rearrange("p t (c i) -> p c t i", i=4),
                 MULT,
             )
 
@@ -279,7 +279,7 @@ def tile_list_htabg_mul_bias_kernel(
 
         last_pick(0)
         last_pick(1)
-        wa_codes = deal("wa_codes", wa_raw[:], RUN)
+        wa_codes = deal(nc.vector, "wa_codes", wa_raw[:], RUN)
         last_pick(2)
         quantise_x(0)
         last_pick(3)

@@ -25,7 +25,6 @@ HEADS = 8
 RUN = 8
 CHUNK = 256
 UNIT = 128
-WIDE = 512
 EARLY_CHUNKS = 3
 VECTOR_BANKS = 3
 GROUPS = (256, 256, 256, 128, 128)
@@ -136,22 +135,22 @@ def tile_list_htabg_mul_bias_kernel(
         x_sb.append(sb("x2", [P, T], F32, tag="big_a"))
         nc.sync.dma_start(out=x_sb[2][:], in_=x_planes[2])
 
+        units = J // UNIT
         yb_sb = []
-        for h in range(J // WIDE):
-            cols = slice(h * WIDE, (h + 1) * WIDE)
-            yb = sb("yb%d" % h, [P, PACK, WIDE], F32)
+        for c in range(units):
+            bank = psum.tile([P, PACK, UNIT], F32, name="ab_bank", bufs=3)
             for t in range(PACK):
-                bank = psum.tile([P, WIDE], F32, name="ab_bank", bufs=3)
                 nc.tensor.matmul_mx(
-                    out=bank[:],
+                    out=bank[:, t, :],
                     lhsT=wb_codes[:, 2 * P * t : 2 * P * (t + 1)].bitcast(FP4X4),
                     lhsT_scale=w_sc[:, P * t : P * (t + 1)],
-                    rhs=v_words[:, cols].bitcast(FP8X4),
-                    rhs_scale=v_scales[:, cols],
+                    rhs=v_words[:, c * UNIT : (c + 1) * UNIT].bitcast(FP8X4),
+                    rhs_scale=v_scales[:, c * UNIT : (c + 1) * UNIT],
                     start=True,
                     stop=True,
                 )
-                nc.scalar.copy(out=yb[:, t, :], in_=bank[:])
+            yb = sb("yb%d" % c, [P, UNIT, PACK], F32)
+            nc.scalar.copy(out=yb[:], in_=bank[:].rearrange("p t j -> p j t"))
             yb_sb.append(yb)
 
         xg = sb("xg", [P, PACK, J], F32)
@@ -214,7 +213,6 @@ def tile_list_htabg_mul_bias_kernel(
 
         def first_stage(u):
             c, c0 = divmod(u * UNIT, CHUNK)
-            h, b0 = divmod(u * UNIT, WIDE)
             bank = psum.tile([P, PACK, UNIT], F32, name="ab_bank", bufs=3)
             for t in range(PACK):
                 nc.tensor.matmul_mx(
@@ -229,9 +227,9 @@ def tile_list_htabg_mul_bias_kernel(
             g = max(n for n in range(len(GROUPS)) if starts[n] <= u * UNIT)
             g0 = (u * UNIT - starts[g]) * PACK
             nc.vector.tensor_tensor(
-                h_bf[g][:, g0 : g0 + UNIT * PACK].rearrange("p (c i t) -> p c t i", i=4, t=PACK),
-                bank[:].rearrange("p t (c i) -> p c t i", i=4),
-                yb_sb[h][:, :, b0 : b0 + UNIT].rearrange("p t (c i) -> p c t i", i=4),
+                h_bf[g][:, g0 : g0 + UNIT * PACK].rearrange("p (j t) -> p j t", t=PACK),
+                bank[:].rearrange("p t j -> p j t"),
+                yb_sb[u][:],
                 MULT,
             )
 

@@ -34,8 +34,8 @@ W_ROW0 = 96
 
 def interleave(nc, dst, src):
     nc.scalar.copy(
-        out=dst.rearrange("p (c i t) -> p c t i", i=4, t=PACK),
-        in_=src.rearrange("p t (c i) -> p c t i", i=4),
+        out=dst.rearrange("p (c i t) -> p c t i", i=2, t=PACK),
+        in_=src.rearrange("p t (c i) -> p c t i", i=2),
     )
 
 
@@ -268,19 +268,21 @@ def tile_list_htabg_mul_bias_kernel(
                         nc.scalar.activation(res[:, s, :], bank[:, s, :], IDENTITY, bias=bias_sb[:, u : u + 1])
                 nc.sync.dma_start(out=out_rows[:, 2 * h : 2 * h + 2, j0 : j0 + w], in_=res[:])
 
-        def last_pick(c):
-            pick(PACK - 1, c * CHUNK, CHUNK)
+        def round_x(c):
             if c < EARLY_CHUNKS:
                 round_pair(c, 2)
             else:
                 interleave(nc, x_bf[c][:], xg[:, :, c * CHUNK : (c + 1) * CHUNK])
 
-        last_pick(0)
-        last_pick(1)
+        pick(PACK - 1, 0, CHUNK)
+        round_x(0)
+        pick(PACK - 1, CHUNK, CHUNK)
+        round_x(1)
         wa_codes = deal(nc.vector, "wa_codes", wa_raw[:], RUN)
-        last_pick(2)
         quantise_x(0)
-        last_pick(3)
+        pick(PACK - 1, 2 * CHUNK, 2 * CHUNK)
+        round_x(2)
+        round_x(3)
         quantise_x(1)
         first_stage(0)
         first_stage(1)

@@ -51,10 +51,10 @@ def tile_list_htabg_mul_bias_kernel(
             return keep.tile(shape, dtype, name=name, tag=tag or name, align_bytes=64)
 
         def move_scale_rows(plane, rows, row0):
-            for q in range(4):
+            for r in range(4):
                 nc.sync.dma_start(
-                    out=plane[32 * q : 32 * q + 4, :].bitcast(I32),
-                    in_=rows[row0 + 4 * q : row0 + 4 * q + 4, :].bitcast(I32),
+                    out=plane[r:P:32, :].bitcast(I32),
+                    in_=rows[row0 + r : row0 + 16 : 4, :].bitcast(I32),
                 )
 
         offs_sb = keep.tile([P, J // LIST_ROWS], U16, name="offs_sb")

@@ -95,6 +95,8 @@ def tile_list_htabg_mul_bias_kernel(
         x_sb = [sb("x0", [P, T], F32, tag="big_b"), sb("x1", [P, T], F32, tag="big_c")]
         nc.sync.dma_start(out=x_sb[0][:], in_=x_planes[0])
         nc.sync.dma_start(offs2_sb[:], offs2)
+        wa_raw = sb("wa_raw", [P, R], U32)
+        nc.sync.dma_start(out=wa_raw[:].bitcast(I32), in_=wa_words[0].rearrange("p r i -> p (r i)").bitcast(I32))
 
         v_scale_rows = sb("v_scale_rows", [P, J], U8)
         nc.vector.tensor_copy(v_scale_rows[:], tab_scale_sb[:].indirect(offs_sb[:]))
@@ -131,6 +133,12 @@ def tile_list_htabg_mul_bias_kernel(
             for c in range(4):
                 nc.tensor.transpose(back[:, c, :], spread[:, 4 * h + c, :], ident[:])
             nc.scalar.copy(out=wgt_sb[:, 512 * h : 512 * (h + 1)], in_=back[:].rearrange("p c k -> p (c k)"))
+
+        wa_codes = sb("wa_codes", [P, 4 * R], U8, tag="ident")
+        nc.scalar.copy(
+            out=wa_codes[:].bitcast(U32).rearrange("p (t a e) -> p t a e", t=PACK, e=RUN),
+            in_=wa_raw[:].rearrange("p (a t e) -> p t a e", t=PACK, e=RUN),
+        )
 
         x_sb.append(sb("x2", [P, T], F32, tag="big_a"))
         nc.sync.dma_start(out=x_sb[2][:], in_=x_planes[2])
@@ -176,9 +184,7 @@ def tile_list_htabg_mul_bias_kernel(
         x_sb.append(sb("x3", [P, T], F32, tag="big_b"))
         nc.sync.dma_start(out=x_sb[3][:], in_=x_planes[3])
         pick(1, 0, J)
-        wa_raw = sb("wa_raw", [P, R], I32, tag="wb_raw")
         wd_raw = sb("wd_raw", [P, PACK, N], F32, tag="big_c")
-        nc.sync.dma_start(out=wa_raw[:], in_=wa_words[0].rearrange("p r i -> p (r i)").bitcast(I32))
         for t in range(PACK):
             nc.sync.dma_start(out=wd_raw[:, t, :], in_=wd_rows[t])
         for c in range(EARLY_CHUNKS):
@@ -278,7 +284,6 @@ def tile_list_htabg_mul_bias_kernel(
         round_x(0)
         pick(PACK - 1, CHUNK, CHUNK)
         round_x(1)
-        wa_codes = deal(nc.vector, "wa_codes", wa_raw[:], RUN)
         quantise_x(0)
         pick(PACK - 1, 2 * CHUNK, 2 * CHUNK)
         round_x(2)

@@ -26,7 +26,7 @@ RUN = 8
 CHUNK = 256
 UNIT = 128
 EARLY_CHUNKS = 3
-VECTOR_BANKS = 3
+VECTOR_BANKS = 2
 GROUPS = (256, 256, 256, 128, 128)
 TAB_ROW0 = 112
 W_ROW0 = 96
@@ -174,8 +174,8 @@ def tile_list_htabg_mul_bias_kernel(
         chunks = J // CHUNK
         x_bf = [sb("x_bf%d" % c, [P, CHUNK * PACK], BF16) for c in range(chunks)]
 
-        def round_pair(c, i0):
-            nc.scalar.copy(
+        def round_pair(c, i0, copy=nc.scalar.copy):
+            copy(
                 out=x_bf[c][:].rearrange("p (j t) -> p j t", t=PACK)[:, :, i0 : i0 + 2],
                 in_=xg[:, i0 : i0 + 2, c * CHUNK : (c + 1) * CHUNK].rearrange("p t j -> p j t"),
             )
@@ -281,12 +281,13 @@ def tile_list_htabg_mul_bias_kernel(
                 interleave(nc, x_bf[c][:], xg[:, :, c * CHUNK : (c + 1) * CHUNK])
 
         pick(PACK - 1, 0, CHUNK)
-        round_x(0)
         pick(PACK - 1, CHUNK, CHUNK)
         round_x(1)
-        quantise_x(0)
-        pick(PACK - 1, 2 * CHUNK, 2 * CHUNK)
+        round_pair(0, 2, nc.vector.tensor_copy)
+        pick(PACK - 1, 2 * CHUNK, CHUNK)
         round_x(2)
+        quantise_x(0)
+        pick(PACK - 1, 3 * CHUNK, CHUNK)
         round_x(3)
         quantise_x(1)
         first_stage(0)

@@ -253,7 +253,10 @@ def tile_list_htabg_mul_bias_kernel(
         def second_stage(g):
             w, j0 = GROUPS[g], starts[g]
             for h in range(2):
-                bank = psum.tile([P, 2, w], F32, name="y_bank", bufs=5)
+                if g == len(GROUPS) - 1:
+                    bank = psum.tile([P, 2, w], F32, name="ab_bank", bufs=3)
+                else:
+                    bank = psum.tile([P, 2, w], F32, name="y_bank", bufs=5)
                 for s in range(2):
                     nc.tensor.matmul_mx(
                         out=bank[:, s, :],
@@ -272,7 +275,10 @@ def tile_list_htabg_mul_bias_kernel(
                     for s in range(2):
                         u = 2 * h + s
                         nc.scalar.activation(res[:, s, :], bank[:, s, :], IDENTITY, bias=bias_sb[:, u : u + 1])
-                nc.sync.dma_start(out=out_rows[:, 2 * h : 2 * h + 2, j0 : j0 + w], in_=res[:])
+                        if g in (1, 2):
+                            nc.sync.dma_start(out=out_rows[:, u, j0 : j0 + w], in_=res[:, s, :])
+                if g not in (1, 2):
+                    nc.sync.dma_start(out=out_rows[:, 2 * h : 2 * h + 2, j0 : j0 + w], in_=res[:])
 
         def round_x(c):
             if c < EARLY_CHUNKS:

@@ -26,7 +26,6 @@ RUN = 8
 CHUNK = 256
 UNIT = 128
 EARLY_CHUNKS = 3
-VECTOR_BANKS = 2
 GROUPS = (256, 256, 256, 128, 128)
 TAB_ROW0 = 112
 W_ROW0 = 96
@@ -268,7 +267,7 @@ def tile_list_htabg_mul_bias_kernel(
                         stop=True,
                     )
                 res = sb("res%d_%d" % (g, h), [P, 2, w], F32)
-                if h == 1 and g >= len(GROUPS) - VECTOR_BANKS:
+                if g == len(GROUPS) - 2 or (g, h) == (len(GROUPS) - 1, 1):
                     wide = bias_sb[:, 2 * h : 2 * h + 2].unsqueeze(2).to_broadcast([P, 2, w])
                     nc.vector.tensor_tensor(res[:], bank[:], wide, ADD)
                 else:

from contextlib import ExitStack

import concourse.mybir as mybir
from concourse.masks import make_identity

K, L, R, N, T, J = 512, 512, 512, 512, 2048, 1024
FLOPS = 2 * J * (K * R + L * R + R * N)

F32 = mybir.dt.float32
BF16 = mybir.dt.bfloat16
I32 = mybir.dt.int32
U32 = mybir.dt.uint32
U16 = mybir.dt.uint16
U8 = mybir.dt.uint8
FP8X4 = mybir.dt.float8_e4m3fn_x4
FP4X4 = mybir.dt.float4_e2m1fn_x4
MULT = mybir.AluOpType.mult
ADD = mybir.AluOpType.add
IDENTITY = mybir.ActivationFunctionType.Identity

P = 128
PACK = 4
LIST_ROWS = 16
HEADS = 8
RUN = 8
CHUNK = 256
UNIT = 128
EARLY_CHUNKS = 3
GROUPS = (256, 256, 256, 128, 128)
TAB_ROW0 = 112
W_ROW0 = 96


def interleave(nc, dst, src):
    nc.scalar.copy(
        out=dst.rearrange("p (c i t) -> p c t i", i=2, t=PACK),
        in_=src.rearrange("p t (c i) -> p c t i", i=2),
    )


def tile_list_htabg_mul_bias_kernel(
    tc, tab_words, tab_scales, xT, wgt2, wa_words, wa_scales, wb_words, wb_scales, wd, b, offs, offs2, out
):
    nc = tc.nc
    with ExitStack() as ctx:
        keep = ctx.enter_context(tc.tile_pool(name="keep", bufs=1))
        psum = ctx.enter_context(tc.psum_pool(name="psum", bufs=4))

        def sb(name, shape, dtype, tag=""):
            return keep.tile(shape, dtype, name=name, tag=tag or name, align_bytes=64)

        def move_scale_rows(plane, rows, row0):
            for r in range(4):
                nc.sync.dma_start(
                    out=plane[r:P:32, :].bitcast(I32),
                    in_=rows[row0 + r : row0 + 16 : 4, :].bitcast(I32),
                )

        offs_sb = keep.tile([P, J // LIST_ROWS], U16, name="offs_sb")
        offs2_sb = keep.tile([P, J // LIST_ROWS], U16, name="offs2_sb")
        tab_scale_sb = sb("tab_scale_sb", [P, T], U8)
        w_scale_raw = sb("w_scale_raw", [P, 2 * R], U8)
        rows_sb = sb("rows_sb", [P, P], F32)
        ident = sb("ident", [P, P], F32)
        tab_word_sb = sb("tab_word_sb", [P, T], U32, tag="big_a")
        wb_raw = sb("wb_raw", [P, R // 2], I32)

        make_identity(nc, ident[:])
        nc.vector.memset(tab_scale_sb[0:96, :].bitcast(I32), 0)
        nc.vector.memset(tab_scale_sb[96:TAB_ROW0, :].bitcast(I32), 0)
        nc.vector.memset(rows_sb[64:P, :], 0.0)

        x_planes = xT.rearrange("(p i) t -> i p t", i=PACK)
        wd_rows = wd.rearrange("(a t e) n -> t a e n", t=PACK, e=RUN)
        wgt_rows = wgt2.rearrange("(g s) (c k) -> s g c k", s=LIST_ROWS, k=P)[0]

        w_rows = w_scale_raw[W_ROW0 : W_ROW0 + 16, :].bitcast(I32)
        nc.sync.dma_start(out=w_rows[:, 0 : R // 4], in_=wb_scales[0].bitcast(I32))
        nc.scalar.dma_start(out=w_rows[:, R // 4 : R // 2], in_=wa_scales[0].bitcast(I32))
        nc.sync.dma_start(offs_sb[:], offs)
        nc.scalar.dma_start(out=tab_scale_sb[TAB_ROW0:P, :].bitcast(I32), in_=tab_scales[0].bitcast(I32))
        nc.sync.dma_start(out=rows_sb[0:64, :], in_=wgt_rows)
        nc.sync.dma_start(out=tab_word_sb[:].bitcast(I32), in_=tab_words[0].rearrange("p t i -> p (t i)").bitcast(I32))
        nc.sync.dma_start(out=wb_raw[:], in_=wb_words[0].bitcast(I32))

        w_scale_dealt = sb("w_scale_dealt", [P, 2 * R], U8)
        nc.vector.tensor_copy(
            out=w_scale_dealt[W_ROW0 : W_ROW0 + 16, :].bitcast(I32).rearrange("p (w t a e) -> p w t a e", w=2, t=PACK, e=RUN // 4),
            in_=w_rows.rearrange("p (w a t e) -> p w t a e", w=2, t=PACK, e=RUN // 4),
        )
        w_sc = sb("w_sc", [P, 2 * R], U8)
        move_scale_rows(w_sc, w_scale_dealt, W_ROW0)

        x_sb = [sb("x0", [P, T], F32, tag="big_b"), sb("x1", [P, T], F32, tag="big_c")]
        nc.sync.dma_start(out=x_sb[0][:], in_=x_planes[0])
        nc.sync.dma_start(offs2_sb[:], offs2)
        wa_raw = sb("wa_raw", [P, R], U32)
        nc.sync.dma_start(out=wa_raw[:].bitcast(I32), in_=wa_words[0].rearrange("p r i -> p (r i)").bitcast(I32))

        v_scale_rows = sb("v_scale_rows", [P, J], U8)
        nc.vector.tensor_copy(v_scale_rows[:], tab_scale_sb[:].indirect(offs_sb[:]))
        v_scales = sb("v_scales", [P, J], U8)
        move_scale_rows(v_scales, v_scale_rows, TAB_ROW0)
        nc.sync.dma_start(out=x_sb[1][:], in_=x_planes[1])

        def deal(engine, name, raw, run):
            width = raw.shape[1]
            dealt = sb(name, [P, 4 * width], U8)
            engine.tensor_copy(
                out=dealt[:].bitcast(I32).rearrange("p (t a e) -> p t a e", t=PACK, e=run),
                in_=raw.rearrange("p (a t e) -> p t a e", t=PACK, e=run),
            )
            return dealt

        wb_codes = deal(nc.gpsimd, "wb_codes", wb_raw[:], RUN // 2)
        v_words = sb("v_words", [P, J], U32)
        nc.vector.tensor_copy(v_words[:], tab_word_sb[:].indirect(offs_sb[:]))

        turned = psum.tile([P, P], F32, name="turned", tag="y_bank", bufs=5)
        nc.tensor.transpose(turned[:], rows_sb[:], ident[:])
        spread = sb("spread", [P, J // P, P], F32)
        wgt_sb = sb("wgt_sb", [P, J], F32)
        by_chunk = turned[:, 0:64].rearrange("p (g c) -> p c g", g=HEADS)
        for h in range(2):
            cs = slice(4 * h, 4 * h + 4)
            nc.scalar.copy(
                out=spread[:, cs, :].rearrange("p c (g s) -> p c g s", g=HEADS),
                in_=by_chunk[:, cs, :].unsqueeze(3).to_broadcast([P, 4, HEADS, LIST_ROWS]),
            )
        for h in range(2):
            back = psum.tile([P, 4, P], F32, name="back", tag="y_bank", bufs=5)
            for c in range(4):
                nc.tensor.transpose(back[:, c, :], spread[:, 4 * h + c, :], ident[:])
            nc.scalar.copy(out=wgt_sb[:, 512 * h : 512 * (h + 1)], in_=back[:].rearrange("p c k -> p (c k)"))

        wa_codes = sb("wa_codes", [P, 4 * R], U8, tag="ident")
        nc.scalar.copy(
            out=wa_codes[:].bitcast(U32).rearrange("p (t a e) -> p t a e", t=PACK, e=RUN),
            in_=wa_raw[:].rearrange("p (a t e) -> p t a e", t=PACK, e=RUN),
        )

        x_sb.append(sb("x2", [P, T], F32, tag="big_a"))
        nc.sync.dma_start(out=x_sb[2][:], in_=x_planes[2])

        units = J // UNIT
        yb_sb = []
        for c in range(units):
            bank = psum.tile([P, PACK, UNIT], F32, name="ab_bank", bufs=3)
            for t in range(PACK):
                nc.tensor.matmul_mx(
                    out=bank[:, t, :],
                    lhsT=wb_codes[:, 2 * P * t : 2 * P * (t + 1)].bitcast(FP4X4),
                    lhsT_scale=w_sc[:, P * t : P * (t + 1)],
                    rhs=v_words[:, c * UNIT : (c + 1) * UNIT].bitcast(FP8X4),
                    rhs_scale=v_scales[:, c * UNIT : (c + 1) * UNIT],
                    start=True,
                    stop=True,
                )
            yb = sb("yb%d" % c, [P, UNIT, PACK], F32)
            nc.scalar.copy(out=yb[:], in_=bank[:].rearrange("p t j -> p j t"))
            yb_sb.append(yb)

        xg = sb("xg", [P, PACK, J], F32)

        def pick(i, j0, width):
            nc.vector.tensor_tensor(
                xg[:, i, j0 : j0 + width],
                x_sb[i][:].indirect(offs2_sb[:, j0 // LIST_ROWS : (j0 + width) // LIST_ROWS]),
                wgt_sb[:, j0 : j0 + width],
                MULT,
            )

        chunks = J // CHUNK
        x_bf = [sb("x_bf%d" % c, [P, CHUNK * PACK], BF16) for c in range(chunks)]

        def round_pair(c, i0, copy=nc.scalar.copy):
            copy(
                out=x_bf[c][:].rearrange("p (j t) -> p j t", t=PACK)[:, :, i0 : i0 + 2],
                in_=xg[:, i0 : i0 + 2, c * CHUNK : (c + 1) * CHUNK].rearrange("p t j -> p j t"),
            )

        pick(0, 0, J)
        x_sb.append(sb("x3", [P, T], F32, tag="big_b"))
        nc.sync.dma_start(out=x_sb[3][:], in_=x_planes[3])
        pick(1, 0, J)
        wd_raw = sb("wd_raw", [P, PACK, N], F32, tag="big_c")
        for t in range(PACK):
            nc.sync.dma_start(out=wd_raw[:, t, :], in_=wd_rows[t])
        for c in range(EARLY_CHUNKS):
            round_pair(c, 0)
        pick(2, 0, J)
        bias_sb = sb("bias_sb", [P, 4], F32, tag="big_a")
        with nc.allow_non_contiguous_dma(reason="one bias value a partition for each block of 128 output rows"):
            nc.sync.dma_start(out=bias_sb[:], in_=b.rearrange("(u m) -> m u", u=4))

        x_codes, x_sc = [], []

        def quantise_x(c):
            codes = sb("x_codes%d" % c, [P, CHUNK], U32)
            sc = sb("x_sc%d" % c, [P, CHUNK], U8)
            nc.vector.quantize_mx(out=codes[:].bitcast(FP8X4), scales=sc[:], in_=x_bf[c][:])
            x_codes.append(codes)
            x_sc.append(sc)

        wd_codes, wd_sc = [], []

        def quantise_wd(h):
            bf = sb("wd_bf%d" % h, [P, N // 2 * PACK], BF16)
            interleave(nc, bf[:], wd_raw[:, :, h * N // 2 : (h + 1) * N // 2])
            codes = sb("wd_codes%d" % h, [P, N // 2], U32)
            sc = sb("wd_sc%d" % h, [P, N // 2], U8)
            nc.vector.quantize_mx(out=codes[:].bitcast(FP8X4), scales=sc[:], in_=bf[:])
            wd_codes.append(codes)
            wd_sc.append(sc)

        starts = [sum(GROUPS[:g]) for g in range(len(GROUPS))]
        h_bf = [sb("h_bf%d" % g, [P, w * PACK], BF16) for g, w in enumerate(GROUPS)]

        def first_stage(u):
            c, c0 = divmod(u * UNIT, CHUNK)
            bank = psum.tile([P, PACK, UNIT], F32, name="ab_bank", bufs=3)
            for t in range(PACK):
                nc.tensor.matmul_mx(
                    out=bank[:, t, :],
                    lhsT=wa_codes[:, 4 * P * t : 4 * P * (t + 1)].bitcast(FP8X4),
                    lhsT_scale=w_sc[:, R + P * t : R + P * (t + 1)],
                    rhs=x_codes[c][:, c0 : c0 + UNIT].bitcast(FP8X4),
                    rhs_scale=x_sc[c][:, c0 : c0 + UNIT],
                    start=True,
                    stop=True,
                )
            g = max(n for n in range(len(GROUPS)) if starts[n] <= u * UNIT)
            g0 = (u * UNIT - starts[g]) * PACK
            nc.vector.tensor_tensor(
                h_bf[g][:, g0 : g0 + UNIT * PACK].rearrange("p (j t) -> p j t", t=PACK),
                bank[:].rearrange("p t j -> p j t"),
                yb_sb[u][:],
                MULT,
            )

        out_rows = out.rearrange("(u m) j -> m u j", m=P)
        h_codes, h_sc = [], []

        def quantise_h(g):
            w = GROUPS[g]
            codes = sb("h_codes%d" % g, [P, w], U32)
            sc = sb("h_sc%d" % g, [P, w], U8)
            nc.vector.quantize_mx(out=codes[:].bitcast(FP8X4), scales=sc[:], in_=h_bf[g][:])
            h_codes.append(codes)
            h_sc.append(sc)

        def second_stage(g):
            w, j0 = GROUPS[g], starts[g]
            for h in range(2):
                if g == len(GROUPS) - 1:
                    bank = psum.tile([P, 2, w], F32, name="ab_bank", bufs=3)
                else:
                    bank = psum.tile([P, 2, w], F32, name="y_bank", bufs=5)
                for s in range(2):
                    nc.tensor.matmul_mx(
                        out=bank[:, s, :],
                        lhsT=wd_codes[h][:, P * s : P * (s + 1)].bitcast(FP8X4),
                        lhsT_scale=wd_sc[h][:, P * s : P * (s + 1)],
                        rhs=h_codes[g][:].bitcast(FP8X4),
                        rhs_scale=h_sc[g][:],
                        start=True,
                        stop=True,
                    )
                res = sb("res%d_%d" % (g, h), [P, 2, w], F32)
                if g == len(GROUPS) - 2 or (g, h) == (len(GROUPS) - 1, 1):
                    wide = bias_sb[:, 2 * h : 2 * h + 2].unsqueeze(2).to_broadcast([P, 2, w])
                    nc.vector.tensor_tensor(res[:], bank[:], wide, ADD)
                else:
                    for s in range(2):
                        u = 2 * h + s
                        nc.scalar.activation(res[:, s, :], bank[:, s, :], IDENTITY, bias=bias_sb[:, u : u + 1])
                        if g in (1, 2):
                            nc.sync.dma_start(out=out_rows[:, u, j0 : j0 + w], in_=res[:, s, :])
                if g not in (1, 2):
                    nc.sync.dma_start(out=out_rows[:, 2 * h : 2 * h + 2, j0 : j0 + w], in_=res[:])

        def round_x(c):
            if c < EARLY_CHUNKS:
                round_pair(c, 2)
            else:
                interleave(nc, x_bf[c][:], xg[:, :, c * CHUNK : (c + 1) * CHUNK])

        pick(PACK - 1, 0, CHUNK)
        pick(PACK - 1, CHUNK, CHUNK)
        round_x(1)
        round_pair(0, 2, nc.vector.tensor_copy)
        pick(PACK - 1, 2 * CHUNK, CHUNK)
        round_x(2)
        quantise_x(0)
        pick(PACK - 1, 3 * CHUNK, CHUNK)
        round_x(3)
        quantise_x(1)
        first_stage(0)
        first_stage(1)
        quantise_x(2)
        first_stage(2)
        quantise_h(0)
        quantise_wd(0)
        first_stage(3)
        quantise_x(3)
        quantise_wd(1)
        second_stage(0)
        first_stage(4)
        quantise_h(1)
        second_stage(1)
        first_stage(5)
        first_stage(6)
        quantise_h(2)
        second_stage(2)
        first_stage(7)
        quantise_h(3)
        second_stage(3)
        quantise_h(4)
        second_stage(4)
